import numpy as np
import ml_dtypes


def mxq(x, axis, fmt="e4m3"):
    dtype, down = {"e4m3": (ml_dtypes.float8_e4m3fn, 7), "e5m2": (ml_dtypes.float8_e5m2, 14)}[fmt]
    v = np.moveaxis(np.asarray(x, np.float32).astype(ml_dtypes.bfloat16).astype(np.float64), axis, -1)
    blocks = v.reshape(v.shape[:-1] + (-1, 32))
    amax = np.abs(blocks).max(-1, keepdims=True)
    byte = np.maximum(np.where(amax > 0, np.frexp(amax)[1] - 1 + 127, 0) - down, 1)
    scale = np.exp2(byte - 127.0)
    codes = (blocks / scale).astype(np.float32).astype(dtype).astype(np.float64)
    return np.moveaxis((codes * scale).reshape(v.shape), -1, axis)


WIDE = False


def mx_kscale(k):
    if not WIDE:
        return np.ones(k)
    levels = np.array([10, -10, 5, -5, 0])
    if k % 512:
        return np.exp2(np.random.permutation(np.resize(levels, k // 32))).repeat(32)
    a = np.empty((k // 512, 16))
    for p in range(k // 512):
        a[p, :8] = np.random.permutation(np.resize(levels, 8))
        for g in range(8):
            far = levels[np.abs(levels - a[p, g]) >= 10]
            a[p, g + 8] = far[np.random.randint(len(far))]
    return np.exp2(a.ravel()).repeat(32)


def f64(x):
    return np.asarray(x).astype(np.float64)


def striped(idx):
    return np.tile(idx.reshape(-1, 16).T, (8, 1)).astype(np.uint16)


def unstriped(offs):
    return offs[:16].T.reshape(-1).astype(np.int64)


E2M1 = np.array([0.0, 0.5, 1.0, 1.5, 2.0, 3.0, 4.0, 6.0, -0.0, -0.5, -1.0, -1.5, -2.0, -3.0, -4.0, -6.0])


def pack_weight(w, fmt):
    k, n = w.shape
    w = f64(np.asarray(w, np.float32).astype(ml_dtypes.bfloat16)).reshape(k // 32, 32, n)
    amax = np.abs(w).max(1)
    if fmt == "e4m3":
        byte = np.frexp(amax)[1] - 1 + 127 - 7
    else:
        mant, ex = np.frexp(amax / 6.0)
        byte = np.where(mant > 0.5, ex, ex - 1) + 127
    byte = np.clip(np.where(amax > 0, byte, 1), 1, 254)
    scaled = (w * np.exp2(127.0 - byte)[:, None, :]).reshape(k, n).astype(np.float32)
    by_word = np.ascontiguousarray(scaled.reshape(k // 512, 128, 4, n).transpose(0, 1, 3, 2))
    if fmt == "e4m3":
        words = by_word.astype(ml_dtypes.float8_e4m3fn).view(np.uint8)
    else:
        c = by_word.astype(ml_dtypes.float4_e2m1fn).view(np.uint8) & 0xF
        words = (c[..., 0::2] | (c[..., 1::2] << 4)).reshape(k // 512, 128, 2 * n)
    return np.ascontiguousarray(words), np.ascontiguousarray(byte.astype(np.uint8).reshape(k // 512, 16, n))


def unpack_weight(words, scales, fmt):
    g, _, n = scales.shape
    words = np.ascontiguousarray(words).reshape(g, 128, n, -1)
    if fmt == "e4m3":
        vals = words.view(ml_dtypes.float8_e4m3fn).astype(np.float64)
    else:
        nib = np.empty((g, 128, n, 4), np.uint8)
        nib[..., 0::2] = words & 0xF
        nib[..., 1::2] = words >> 4
        vals = E2M1[nib]
    vals = vals * np.repeat(np.exp2(scales.astype(np.float64) - 127.0), 8, axis=1)[..., None]
    return vals.transpose(0, 1, 3, 2).reshape(g * 512, n)


def gelu(v):
    return 0.5 * v * (1.0 + np.tanh(np.sqrt(2.0 / np.pi) * (v + 0.044715 * v**3)))


def bf(x):
    return np.asarray(x, np.float32).astype(ml_dtypes.bfloat16)


def planes(Y):
    n, m = Y.shape
    b = f64(bf(Y)).reshape(n // 32, 32, m)
    amax = np.abs(b).max(1)
    byte = np.clip(np.where(amax > 0, np.frexp(amax)[1] - 1 + 127 - 7, 1), 1, 254)
    codes = (b * np.exp2(127.0 - byte)[:, None, :]).reshape(n, m).astype(np.float32).astype(ml_dtypes.float8_e4m3fn).view(np.uint8)
    words = codes.reshape(n // 512, 128, 4, m).transpose(0, 1, 3, 2)
    return np.ascontiguousarray(words), np.ascontiguousarray(byte.astype(np.uint8).reshape(n // 512, 16, m))


T, S, K, H, N, P = 4096, 1024, 1536, 1024, 512, 512

def setup_inputs():
    n = np.random.standard_normal
    s = mx_kscale(K)[:, None]
    u = mx_kscale(H)[:, None]
    cs = np.exp(0.8 * n(N))
    d = {}
    d["tab_words"], d["tab_scales"] = pack_weight(n((K, T)) * s, "e4m3")
    d["offs"] = striped(np.random.permutation(T)[:S])
    d["w1"] = (1.4 * n((K, H)) / K ** 0.5 / s).astype(np.float32)
    d["gain"] = (2.5 * np.exp(0.3 * n(H)) * u[:, 0]).astype(np.float32)
    d["w4_words"], d["w4_scales"] = pack_weight(n((H, N)) / H ** 0.5 / u * cs[None, :], "e2m1")
    d["pos1"] = striped(np.random.permutation(S)[:P])
    d["pos2"] = striped(np.random.permutation(S)[:P])
    d["base"] = (0.6 * n((N, P)) * cs[:, None]).astype(np.float32)
    return d

def reference(tab_words, tab_scales, offs, w1, gain, w4_words, w4_scales, pos1, pos2, base):
    v = unpack_weight(tab_words, tab_scales, "e4m3")[:, unstriped(offs)]
    w4 = unpack_weight(w4_words, w4_scales, "e2m1")
    a = mxq(f64(w1), 0, "e4m3").T @ v
    h = f64(gain)[:, None] * a / (1.0 + np.square(a))
    e = w4.T @ mxq(h, 0, "e4m3")
    g2 = e / (1.0 + np.exp(-e))
    y = np.minimum(g2[:, unstriped(pos1)], g2[:, unstriped(pos2)]) - f64(base)
    words, scales = planes(y)
    return y, words, scales

@@ -1,0 +1,310 @@
+from contextlib import ExitStack
+
+import concourse.mybir as mybir
+
+T, S, K, H, N, P = 4096, 1024, 1536, 1024, 512, 512
+FLOPS = 2 * K * H * S + 2 * H * N * S
+
+F32 = mybir.dt.float32
+BF16 = mybir.dt.bfloat16
+I32 = mybir.dt.int32
+U32 = mybir.dt.uint32
+U16 = mybir.dt.uint16
+U8 = mybir.dt.uint8
+FP8X4 = mybir.dt.float8_e4m3fn_x4
+FP4X4 = mybir.dt.float4_e2m1fn_x4
+ACT = mybir.ActivationFunctionType
+ALU = mybir.AluOpType
+
+PART = 128
+KP = K // 512
+HP = H // 512
+HALF = 512
+PAIR_CHUNKS = ((0, 384), (384, 128))
+
+
+def tile_list_kiln_pair_minimum_kernel(
+    tc, tab_words, tab_scales, offs, w1, gain, w4_words, w4_scales, pos1, pos2, base, out_0, out_1, out_2
+):
+    nc = tc.nc
+    with ExitStack() as ctx:
+        keep = ctx.enter_context(tc.tile_pool(name="keep", bufs=1))
+        work = ctx.enter_context(tc.tile_pool(name="work", bufs=2))
+        tail = ctx.enter_context(tc.tile_pool(name="tail", bufs=1))
+        psum = ctx.enter_context(tc.psum_pool(name="psum", bufs=8))
+
+        idx = keep.tile([PART, S // 16], U16, name="idx")
+        p1 = keep.tile([PART, P // 16], U16, name="p1")
+        p2 = keep.tile([PART, P // 16], U16, name="p2")
+        g = keep.tile([PART, HP, 4], F32, name="g")
+        v_codes = [keep.tile([PART, S], U32, name="v_codes%d" % a, align_bytes=64) for a in range(KP)]
+        v_scales = keep.tile([PART, S], U8, name="v_scales", align_bytes=64)
+        w1_codes = {}
+        w1_scales = {}
+        for b in range(HP):
+            for a in range(KP):
+                w1_codes[b, a] = keep.tile([PART, 512], U32, name="w1_codes%d%d" % (b, a), align_bytes=64)
+                w1_scales[b, a] = keep.tile([PART, 512], U8, name="w1_scales%d%d" % (b, a), align_bytes=64)
+        w4_codes = keep.tile([PART, HP * 1024], U8, name="w4_codes", align_bytes=64)
+        w4_planes = keep.tile([PART, HP * 512], U8, name="w4_planes", align_bytes=64)
+        h_codes = {}
+        h_scales = {}
+        for b in range(HP):
+            for c in range(2):
+                h_codes[b, c] = keep.tile([PART, HALF], U32, name="h_codes%d%d" % (b, c), align_bytes=64)
+                h_scales[b, c] = keep.tile([PART, HALF], U8, name="h_scales%d%d" % (b, c), align_bytes=64)
+        warm_in = keep.tile([PART, 1], F32, name="warm_in")
+        warm_out = keep.tile([PART, 1], F32, name="warm_out")
+
+        banks = {}
+        hb_tiles = {}
+
+        def first_product(b, c, a):
+            for t in range(4):
+                if a == 0:
+                    banks[b, c, t] = psum.tile([PART, HALF], F32, name="bank", tag="bank")
+                cols = slice(c * HALF, (c + 1) * HALF)
+                nc.tensor.matmul_mx(
+                    out=banks[b, c, t][:],
+                    lhsT=w1_codes[b, a][:, t * 128 : (t + 1) * 128].bitcast(FP8X4),
+                    lhsT_scale=w1_scales[b, a][:, t * 128 : (t + 1) * 128],
+                    rhs=v_codes[a][:, cols].bitcast(FP8X4),
+                    rhs_scale=v_scales[4 * a : PART, cols],
+                    start=(a == 0),
+                    stop=(a == KP - 1),
+                )
+
+        def response_parts(b, c, last):
+            rs = work.tile([PART, 4, HALF], F32, name="rs", tag="rs")
+            u = work.tile([PART, 4, HALF], F32, name="u", tag="u")
+            if last:
+                q_last = tail.tile([PART, 4 * S], F32, name="q_last", offset=0)
+
+            def part(t):
+                if last:
+                    q = q_last[:, t * HALF : (t + 1) * HALF]
+                else:
+                    q = work.tile([PART, HALF], F32, name="q", tag="q", bufs=3)[:]
+                nc.scalar.activation(out=q, in_=banks[b, c, t][:], func=ACT.Square)
+                nc.scalar.activation(out=rs[:, t, :], in_=q, func=ACT.Abs_reciprocal_sqrt, bias=1.0, scale=1.0)
+                nc.vector.scalar_tensor_tensor(
+                    out=u[:, t, :], in0=banks[b, c, t][:], scalar=g[:, b, t : t + 1], in1=rs[:, t, :],
+                    op0=ALU.mult, op1=ALU.mult,
+                )
+
+            def finish():
+                hb = work.tile([PART, 4 * HALF], BF16, name="hb", tag="hb", align_bytes=64)
+                hb_tiles[b, c] = hb
+                nc.vector.tensor_tensor(
+                    out=hb[:].rearrange("p (m i t) -> p m t i", i=2, t=4),
+                    in0=u[:].rearrange("p t (m i) -> p m t i", i=2),
+                    in1=rs[:].rearrange("p t (m i) -> p m t i", i=2),
+                    op=ALU.mult,
+                )
+
+            return part, finish
+
+        def quantise_h(b, c):
+            nc.vector.quantize_mx(out=h_codes[b, c][:].bitcast(FP8X4), scales=h_scales[b, c][:], in_=hb_tiles[b, c][:])
+
+        def second_product(t, c, b):
+            if b == 0:
+                banks["e", c, t] = psum.tile([PART, HALF], F32, name="bank", tag="bank")
+            col = b * 512 + t * 128
+            nc.tensor.matmul_mx(
+                out=banks["e", c, t][:],
+                lhsT=w4_codes[:, 2 * col : 2 * col + 256].bitcast(FP4X4),
+                lhsT_scale=w4_planes[:, col : col + 128],
+                rhs=h_codes[b, c][:].bitcast(FP8X4),
+                rhs_scale=h_scales[b, c][:],
+                start=(b == 0),
+                stop=(b == HP - 1),
+            )
+
+        with ExitStack() as early_ctx:
+            early = early_ctx.enter_context(tc.tile_pool(name="early", bufs=1))
+            tab = [early.tile([PART, T], I32, name="tab%d" % a) for a in range(KP)]
+            tab_planes = early.tile([PART, T], U8, name="tab_planes")
+            w4_raw = early.tile([PART, HP * 1024], U8, name="w4_raw")
+            w4_raw_planes = early.tile([PART, HP * 512], U8, name="w4_raw_planes")
+            raw = {}
+            for b in range(HP):
+                for a in range(KP):
+                    raw[b, a] = early.tile([PART, 4, 512], F32, name="raw%d%d" % (b, a))
+            rounded = {}
+
+            def load_w1(b, a):
+                rows = w1[a * 512 : (a + 1) * 512, b * 512 : (b + 1) * 512]
+                nc.sync.dma_start(out=raw[b, a][:], in_=rows.rearrange("(p j) r -> p j r", j=4))
+
+            def round_w1(b, a, copy):
+                wb = early.tile([PART, 2048], BF16, name="wb", tag="wb", bufs=3, align_bytes=64)
+                rounded[b, a] = wb
+                copy(
+                    out=wb[:].rearrange("p (u e m j) -> p u m j e", u=2, e=2, j=4),
+                    in_=raw[b, a][:].rearrange("p j (m u e) -> p u m j e", u=2, e=2),
+                )
+
+            def quantise_w1(b, a):
+                nc.vector.quantize_mx(
+                    out=w1_codes[b, a][:].bitcast(FP8X4), scales=w1_scales[b, a][:], in_=rounded[b, a][:]
+                )
+
+            def gather_words(a, lo, hi):
+                nc.vector.tensor_copy(
+                    out=v_codes[a][:, lo:hi], in_=tab[a][:].bitcast(U32).indirect(idx[:, lo // 16 : hi // 16])
+                )
+
+            nc.vector.memset(tab_planes[:].bitcast(I32), 0)
+            nc.vector.memset(w4_raw_planes[:].bitcast(I32), 0)
+            nc.vector.memset(warm_in[:], 1.0)
+            nc.scalar.activation(out=warm_out[:], in_=warm_in[:], func=ACT.Abs_reciprocal_sqrt, bias=1.0, scale=1.0)
+
+            load_w1(0, 0)
+            for quad in range(4):
+                nc.sync.dma_start(
+                    out=tab_planes[32 * quad : 32 * quad + 4 * KP, :].bitcast(I32),
+                    in_=tab_scales[:, 4 * quad : 4 * quad + 4, :].bitcast(I32),
+                )
+            nc.sync.dma_start(idx[:], offs)
+            for a in range(1, KP):
+                load_w1(0, a)
+            nc.sync.dma_start(
+                out=w4_raw[:].bitcast(I32).rearrange("p (b n) -> p b n", b=HP),
+                in_=w4_words.bitcast(I32).rearrange("b p n -> p b n"),
+            )
+            for quad in range(4):
+                nc.sync.dma_start(
+                    out=w4_raw_planes[32 * quad : 32 * quad + 4, :].bitcast(I32).rearrange("p (b n) -> p b n", b=HP),
+                    in_=w4_scales[:, 4 * quad : 4 * quad + 4, :].bitcast(I32).rearrange("b r n -> r b n"),
+                )
+            for a in range(KP):
+                nc.sync.dma_start(out=tab[a][:], in_=tab_words[a].rearrange("p t i -> p (t i)").bitcast(I32))
+            nc.sync.dma_start(out=g[:], in_=gain.rearrange("(b p t) -> p b t", b=HP, t=4))
+            for a in range(KP):
+                load_w1(1, a)
+            nc.sync.dma_start(p1[:], pos1)
+            nc.sync.dma_start(p2[:], pos2)
+
+            for a in range(KP):
+                round_w1(0, a, nc.scalar.copy)
+                quantise_w1(0, a)
+            nc.vector.tensor_copy(out=v_scales[:], in_=tab_planes[:].indirect(idx[:]))
+            nc.vector.tensor_copy(
+                out=w4_codes[:].rearrange("p (b t q e) -> p b t q e", b=HP, t=4, e=2),
+                in_=w4_raw[:].rearrange("p (b q t e) -> p b t q e", b=HP, t=4, e=2),
+            )
+            nc.vector.tensor_copy(
+                out=w4_planes[:].rearrange("p (b t q) -> p b t q", b=HP, t=4),
+                in_=w4_raw_planes[:].rearrange("p (b q t) -> p b t q", b=HP, t=4),
+            )
+            for a in range(KP - 1):
+                gather_words(a, 0, S)
+                first_product(0, 0, a)
+                first_product(0, 1, a)
+            gather_words(KP - 1, 0, HALF)
+            first_product(0, 0, KP - 1)
+            gather_words(KP - 1, HALF, S)
+            first_product(0, 1, KP - 1)
+
+            part, finish = response_parts(0, 0, False)
+            for t in range(4):
+                part(t)
+            round_w1(1, 0, nc.scalar.copy)
+            finish()
+            round_w1(1, 1, nc.scalar.copy)
+            quantise_w1(1, 0)
+            quantise_h(0, 0)
+            round_w1(1, 2, nc.vector.tensor_copy)
+            quantise_w1(1, 1)
+            part, finish = response_parts(0, 1, False)
+            part(0)
+            quantise_w1(1, 2)
+            for t in range(1, 4):
+                part(t)
+            finish()
+
+        late = ctx.enter_context(tc.tile_pool(name="late", bufs=1))
+        base_rows = base.rearrange("(p t) m -> p t m", t=4)
+        out_rows = out_0.rearrange("(p t) m -> p t m", t=4)
+        base_tiles = []
+        for m0, width in PAIR_CHUNKS:
+            tile = late.tile([PART, 4, width], F32, name="base%d" % m0)
+            nc.sync.dma_start(out=tile[:], in_=base_rows[:, :, m0 : m0 + width])
+            base_tiles.append(tile)
+
+        for a in range(KP):
+            first_product(1, 0, a)
+        part, finish = response_parts(1, 0, False)
+        part(0)
+        quantise_h(0, 1)
+        for t in range(1, 4):
+            part(t)
+        finish()
+        for a in range(KP):
+            first_product(1, 1, a)
+        part, finish = response_parts(1, 1, True)
+        part(0)
+        quantise_h(1, 0)
+        for t in range(4):
+            for b in range(HP):
+                second_product(t, 0, b)
+        for t in range(1, 4):
+            part(t)
+        finish()
+        for t in range(4):
+            second_product(t, 1, 0)
+        quantise_h(1, 1)
+        g2 = []
+        for t in range(4):
+            g2.append(tail.tile([PART, S], F32, name="g2_%d" % t, offset=t * S * 4))
+            nc.scalar.activation(out=g2[t][:, 0:HALF], in_=banks["e", 0, t][:], func=ACT.Silu)
+        for t in range(4):
+            second_product(t, 1, 1)
+            nc.scalar.activation(out=g2[t][:, HALF:S], in_=banks["e", 1, t][:], func=ACT.Silu)
+
+        y_codes = late.tile([PART, P], U32, name="y_codes", align_bytes=64)
+        y_scales = late.tile([PART, P], U8, name="y_scales", align_bytes=64)
+        words_out = out_1[0].rearrange("p m t -> p (m t)").bitcast(I32)
+        pending = []
+        for chunk, (m0, width) in enumerate(PAIR_CHUNKS):
+            left = late.tile([PART, 4, width], F32, name="left%d" % m0)
+            right = late.tile([PART, 4, width], F32, name="right%d" % m0)
+            y = late.tile([PART, 4, width], F32, name="y%d" % m0)
+            yb = late.tile([PART, 4 * width], BF16, name="yb%d" % m0, align_bytes=64)
+            cols = slice(m0 // 16, (m0 + width) // 16)
+            for t in range(4):
+                nc.vector.tensor_copy(out=left[:, t, :], in_=g2[t][:].indirect(p1[:, cols]))
+                nc.vector.tensor_copy(out=right[:, t, :], in_=g2[t][:].indirect(p2[:, cols]))
+            for step in pending:
+                step()
+            nc.vector.tensor_tensor(out=left[:], in0=left[:], in1=right[:], op=ALU.min)
+            nc.vector.tensor_tensor(out=y[:], in0=left[:], in1=base_tiles[chunk][:], op=ALU.subtract)
+            nc.sync.dma_start(out=out_rows[:, :, m0 : m0 + width], in_=y[:])
+            copy = nc.vector.tensor_copy if chunk == len(PAIR_CHUNKS) - 1 else nc.scalar.copy
+            copy(
+                out=yb[:].rearrange("p (m i t) -> p m t i", i=2, t=4),
+                in_=y[:].rearrange("p t (m i) -> p m t i", i=2),
+            )
+
+            def planes(m0=m0, width=width, yb=yb):
+                done = 0
+                for piece in (256, 128):
+                    if done + piece <= width:
+                        lo = m0 + done
+                        nc.vector.quantize_mx(
+                            out=y_codes[:, lo : lo + piece].bitcast(FP8X4),
+                            scales=y_scales[:, lo : lo + piece],
+                            in_=yb[:, 4 * done : 4 * (done + piece)],
+                        )
+                        done = done + piece
+                nc.sync.dma_start(out=words_out[:, m0 : m0 + width], in_=y_codes[:, m0 : m0 + width].bitcast(I32))
+
+            pending = [planes]
+        for step in pending:
+            step()
+        for quad in range(4):
+            nc.scalar.dma_start(
+                out=out_2[0][4 * quad : 4 * quad + 4, :].bitcast(I32),
+                in_=y_scales[32 * quad : 32 * quad + 4, :].bitcast(I32),
+            )

@@ -59,53 +59,69 @@ def tile_list_kiln_pair_minimum_kernel(
         banks = {}
         hb_tiles = {}
 
-        def first_product(b, c, a):
+        def first_product(b, col0, width, passes):
+            per_bank = HALF // width
+            cols = slice(col0, col0 + width)
             for t in range(4):
-                if a == 0:
-                    banks[b, c, t] = psum.tile([PART, HALF], F32, name="bank", tag="bank")
-                cols = slice(c * HALF, (c + 1) * HALF)
-                nc.tensor.matmul_mx(
-                    out=banks[b, c, t][:],
-                    lhsT=w1_codes[b, a][:, t * 128 : (t + 1) * 128].bitcast(FP8X4),
-                    lhsT_scale=w1_scales[b, a][:, t * 128 : (t + 1) * 128],
-                    rhs=v_codes[a][:, cols].bitcast(FP8X4),
-                    rhs_scale=v_scales[4 * a : PART, cols],
-                    start=(a == 0),
-                    stop=(a == KP - 1),
-                )
+                for a in passes:
+                    if a == 0 and t % per_bank == 0:
+                        banks[b, col0, t // per_bank] = psum.tile([PART, HALF], F32, name="bank", tag="bank")
+                    place = (t % per_bank) * width
+                    nc.tensor.matmul_mx(
+                        out=banks[b, col0, t // per_bank][:, place : place + width],
+                        lhsT=w1_codes[b, a][:, t * 128 : (t + 1) * 128].bitcast(FP8X4),
+                        lhsT_scale=w1_scales[b, a][:, t * 128 : (t + 1) * 128],
+                        rhs=v_codes[a][:, cols].bitcast(FP8X4),
+                        rhs_scale=v_scales[4 * a : PART, cols],
+                        start=(a == 0),
+                        stop=(a == KP - 1),
+                    )
 
-        def response_parts(b, c, last):
-            rs = work.tile([PART, 4, HALF], F32, name="rs", tag="rs")
-            u = work.tile([PART, 4, HALF], F32, name="u", tag="u")
-            if last:
-                q_last = tail.tile([PART, 4 * S], F32, name="q_last", offset=0)
+        def response_parts(b, col0, width, squares=None):
+            per_bank = HALF // width
+            rs = work.tile([PART, 4 * width], F32, name="rs", tag="rs")
+            u = work.tile([PART, 4 * width], F32, name="u", tag="u")
 
-            def part(t):
-                if last:
-                    q = q_last[:, t * HALF : (t + 1) * HALF]
-                else:
+            def part(n):
+                bank = banks[b, col0, n]
+                if squares is None:
                     q = work.tile([PART, HALF], F32, name="q", tag="q", bufs=3)[:]
-                nc.scalar.activation(out=q, in_=banks[b, c, t][:], func=ACT.Square)
-                nc.scalar.activation(out=rs[:, t, :], in_=q, func=ACT.Abs_reciprocal_sqrt, bias=1.0, scale=1.0)
-                nc.vector.scalar_tensor_tensor(
-                    out=u[:, t, :], in0=banks[b, c, t][:], scalar=g[:, b, t : t + 1], in1=rs[:, t, :],
-                    op0=ALU.mult, op1=ALU.mult,
+                else:
+                    q = squares[:, n * HALF : (n + 1) * HALF]
+                nc.scalar.activation(out=q, in_=bank[:], func=ACT.Square)
+                nc.scalar.activation(
+                    out=rs[:, n * HALF : (n + 1) * HALF], in_=q, func=ACT.Abs_reciprocal_sqrt, bias=1.0, scale=1.0
                 )
+                for t in range(n * per_bank, (n + 1) * per_bank):
+                    place = (t % per_bank) * width
+                    nc.vector.scalar_tensor_tensor(
+                        out=u[:, t * width : (t + 1) * width],
+                        in0=bank[:, place : place + width],
+                        scalar=g[:, b, t : t + 1],
+                        in1=rs[:, t * width : (t + 1) * width],
+                        op0=ALU.mult,
+                        op1=ALU.mult,
+                    )
 
             def finish():
-                hb = work.tile([PART, 4 * HALF], BF16, name="hb", tag="hb", align_bytes=64)
-                hb_tiles[b, c] = hb
+                hb = work.tile([PART, 4 * width], BF16, name="hb", tag="hb", align_bytes=64)
+                hb_tiles[b, col0] = hb
                 nc.vector.tensor_tensor(
                     out=hb[:].rearrange("p (m i t) -> p m t i", i=2, t=4),
-                    in0=u[:].rearrange("p t (m i) -> p m t i", i=2),
-                    in1=rs[:].rearrange("p t (m i) -> p m t i", i=2),
+                    in0=u[:].rearrange("p (t m i) -> p m t i", t=4, i=2),
+                    in1=rs[:].rearrange("p (t m i) -> p m t i", t=4, i=2),
                     op=ALU.mult,
                 )
 
             return part, finish
 
-        def quantise_h(b, c):
-            nc.vector.quantize_mx(out=h_codes[b, c][:].bitcast(FP8X4), scales=h_scales[b, c][:], in_=hb_tiles[b, c][:])
+        def quantise_h(b, col0, width):
+            c, lo = divmod(col0, HALF)
+            nc.vector.quantize_mx(
+                out=h_codes[b, c][:, lo : lo + width].bitcast(FP8X4),
+                scales=h_scales[b, c][:, lo : lo + width],
+                in_=hb_tiles[b, col0][:],
+            )
 
         def second_product(t, c, b):
             if b == 0:
@@ -160,15 +176,19 @@ def tile_list_kiln_pair_minimum_kernel(
             nc.vector.memset(warm_in[:], 1.0)
             nc.scalar.activation(out=warm_out[:], in_=warm_in[:], func=ACT.Abs_reciprocal_sqrt, bias=1.0, scale=1.0)
 
+            def load_tab(a):
+                nc.sync.dma_start(out=tab[a][:], in_=tab_words[a].rearrange("p t i -> p (t i)").bitcast(I32))
+
             load_w1(0, 0)
+            load_w1(0, 1)
             for quad in range(4):
                 nc.sync.dma_start(
                     out=tab_planes[32 * quad : 32 * quad + 4 * KP, :].bitcast(I32),
                     in_=tab_scales[:, 4 * quad : 4 * quad + 4, :].bitcast(I32),
                 )
             nc.sync.dma_start(idx[:], offs)
-            for a in range(1, KP):
-                load_w1(0, a)
+            load_w1(0, 2)
+            load_tab(0)
             nc.sync.dma_start(
                 out=w4_raw[:].bitcast(I32).rearrange("p (b n) -> p b n", b=HP),
                 in_=w4_words.bitcast(I32).rearrange("b p n -> p b n"),
@@ -178,8 +198,8 @@ def tile_list_kiln_pair_minimum_kernel(
                     out=w4_raw_planes[32 * quad : 32 * quad + 4, :].bitcast(I32).rearrange("p (b n) -> p b n", b=HP),
                     in_=w4_scales[:, 4 * quad : 4 * quad + 4, :].bitcast(I32).rearrange("b r n -> r b n"),
                 )
-            for a in range(KP):
-                nc.sync.dma_start(out=tab[a][:], in_=tab_words[a].rearrange("p t i -> p (t i)").bitcast(I32))
+            load_tab(1)
+            load_tab(2)
             nc.sync.dma_start(out=g[:], in_=gain.rearrange("(b p t) -> p b t", b=HP, t=4))
             for a in range(KP):
                 load_w1(1, a)
@@ -190,6 +210,10 @@ def tile_list_kiln_pair_minimum_kernel(
                 round_w1(0, a, nc.scalar.copy)
                 quantise_w1(0, a)
             nc.vector.tensor_copy(out=v_scales[:], in_=tab_planes[:].indirect(idx[:]))
+            for a in range(KP - 1):
+                gather_words(a, 0, S)
+                first_product(0, 0, HALF, [a])
+                first_product(0, HALF, HALF, [a])
             nc.vector.tensor_copy(
                 out=w4_codes[:].rearrange("p (b t q e) -> p b t q e", b=HP, t=4, e=2),
                 in_=w4_raw[:].rearrange("p (b q t e) -> p b t q e", b=HP, t=4, e=2),
@@ -198,26 +222,22 @@ def tile_list_kiln_pair_minimum_kernel(
                 out=w4_planes[:].rearrange("p (b t q) -> p b t q", b=HP, t=4),
                 in_=w4_raw_planes[:].rearrange("p (b q t) -> p b t q", b=HP, t=4),
             )
-            for a in range(KP - 1):
-                gather_words(a, 0, S)
-                first_product(0, 0, a)
-                first_product(0, 1, a)
             gather_words(KP - 1, 0, HALF)
-            first_product(0, 0, KP - 1)
+            first_product(0, 0, HALF, [KP - 1])
             gather_words(KP - 1, HALF, S)
-            first_product(0, 1, KP - 1)
+            first_product(0, HALF, HALF, [KP - 1])
 
-            part, finish = response_parts(0, 0, False)
+            part, finish = response_parts(0, 0, HALF)
             for t in range(4):
                 part(t)
-            round_w1(1, 0, nc.scalar.copy)
-            finish()
+            round_w1(1, 0, nc.vector.tensor_copy)
             round_w1(1, 1, nc.scalar.copy)
+            finish()
             quantise_w1(1, 0)
-            quantise_h(0, 0)
-            round_w1(1, 2, nc.vector.tensor_copy)
+            round_w1(1, 2, nc.scalar.copy)
+            quantise_h(0, 0, HALF)
             quantise_w1(1, 1)
-            part, finish = response_parts(0, 1, False)
+            part, finish = response_parts(0, HALF, HALF)
             part(0)
             quantise_w1(1, 2)
             for t in range(1, 4):
@@ -233,28 +253,32 @@ def tile_list_kiln_pair_minimum_kernel(
             nc.sync.dma_start(out=tile[:], in_=base_rows[:, :, m0 : m0 + width])
             base_tiles.append(tile)
 
-        for a in range(KP):
-            first_product(1, 0, a)
-        part, finish = response_parts(1, 0, False)
+        first_product(1, 0, HALF, range(KP))
+        part, finish = response_parts(1, 0, HALF)
         part(0)
-        quantise_h(0, 1)
+        quantise_h(0, HALF, HALF)
         for t in range(1, 4):
             part(t)
         finish()
-        for a in range(KP):
-            first_product(1, 1, a)
-        part, finish = response_parts(1, 1, True)
+        first_product(1, HALF, 256, range(KP))
+        first_product(1, HALF + 256, 256, range(KP))
+        part, finish = response_parts(1, HALF, 256)
         part(0)
-        quantise_h(1, 0)
+        quantise_h(1, 0, HALF)
         for t in range(4):
             for b in range(HP):
                 second_product(t, 0, b)
-        for t in range(1, 4):
-            part(t)
+        part(1)
+        finish()
+        q_last = tail.tile([PART, 4 * S], F32, name="q_last", offset=0)
+        part, finish = response_parts(1, HALF + 256, 256, q_last)
+        part(0)
+        quantise_h(1, HALF, 256)
+        part(1)
         finish()
         for t in range(4):
             second_product(t, 1, 0)
-        quantise_h(1, 1)
+        quantise_h(1, HALF + 256, 256)
         g2 = []
         for t in range(4):
             g2.append(tail.tile([PART, S], F32, name="g2_%d" % t, offset=t * S * 4))
@@ -274,12 +298,12 @@ def tile_list_kiln_pair_minimum_kernel(
             yb = late.tile([PART, 4 * width], BF16, name="yb%d" % m0, align_bytes=64)
             cols = slice(m0 // 16, (m0 + width) // 16)
             for t in range(4):
-                nc.vector.tensor_copy(out=left[:, t, :], in_=g2[t][:].indirect(p1[:, cols]))
-                nc.vector.tensor_copy(out=right[:, t, :], in_=g2[t][:].indirect(p2[:, cols]))
+                given = base_tiles[chunk][:, t, :]
+                nc.vector.tensor_tensor(out=left[:, t, :], in0=g2[t][:].indirect(p1[:, cols]), in1=given, op=ALU.subtract)
+                nc.vector.tensor_tensor(out=right[:, t, :], in0=g2[t][:].indirect(p2[:, cols]), in1=given, op=ALU.subtract)
             for step in pending:
                 step()
-            nc.vector.tensor_tensor(out=left[:], in0=left[:], in1=right[:], op=ALU.min)
-            nc.vector.tensor_tensor(out=y[:], in0=left[:], in1=base_tiles[chunk][:], op=ALU.subtract)
+            nc.vector.tensor_tensor(out=y[:], in0=left[:], in1=right[:], op=ALU.min)
             nc.sync.dma_start(out=out_rows[:, :, m0 : m0 + width], in_=y[:])
             copy = nc.vector.tensor_copy if chunk == len(PAIR_CHUNKS) - 1 else nc.scalar.copy
             copy(
@@ -304,7 +328,8 @@ def tile_list_kiln_pair_minimum_kernel(
         for step in pending:
             step()
         for quad in range(4):
-            nc.scalar.dma_start(
+            queue = nc.sync if quad < 2 else nc.scalar
+            queue.dma_start(
                 out=out_2[0][4 * quad : 4 * quad + 4, :].bitcast(I32),
                 in_=y_scales[32 * quad : 32 * quad + 4, :].bitcast(I32),
             )

from contextlib import ExitStack

import concourse.mybir as mybir

T, S, K, H, N, P = 4096, 1024, 1536, 1024, 512, 512
FLOPS = 2 * K * H * S + 2 * H * N * S

F32 = mybir.dt.float32
BF16 = mybir.dt.bfloat16
I32 = mybir.dt.int32
U32 = mybir.dt.uint32
U16 = mybir.dt.uint16
U8 = mybir.dt.uint8
FP8X4 = mybir.dt.float8_e4m3fn_x4
FP4X4 = mybir.dt.float4_e2m1fn_x4
ACT = mybir.ActivationFunctionType
ALU = mybir.AluOpType

PART = 128
KP = K // 512
HP = H // 512
HALF = 512
PAIR_CHUNKS = ((0, 384), (384, 128))


def tile_list_kiln_pair_minimum_kernel(
    tc, tab_words, tab_scales, offs, w1, gain, w4_words, w4_scales, pos1, pos2, base, out_0, out_1, out_2
):
    nc = tc.nc
    with ExitStack() as ctx:
        keep = ctx.enter_context(tc.tile_pool(name="keep", bufs=1))
        work = ctx.enter_context(tc.tile_pool(name="work", bufs=2))
        tail = ctx.enter_context(tc.tile_pool(name="tail", bufs=1))
        psum = ctx.enter_context(tc.psum_pool(name="psum", bufs=8))

        idx = keep.tile([PART, S // 16], U16, name="idx")
        p1 = keep.tile([PART, P // 16], U16, name="p1")
        p2 = keep.tile([PART, P // 16], U16, name="p2")
        g = keep.tile([PART, HP, 4], F32, name="g")
        v_codes = [keep.tile([PART, S], U32, name="v_codes%d" % a, align_bytes=64) for a in range(KP)]
        v_scales = keep.tile([PART, S], U8, name="v_scales", align_bytes=64)
        w1_codes = {}
        w1_scales = {}
        for b in range(HP):
            for a in range(KP):
                w1_codes[b, a] = keep.tile([PART, 512], U32, name="w1_codes%d%d" % (b, a), align_bytes=64)
                w1_scales[b, a] = keep.tile([PART, 512], U8, name="w1_scales%d%d" % (b, a), align_bytes=64)
        w4_codes = keep.tile([PART, HP * 1024], U8, name="w4_codes", align_bytes=64)
        w4_planes = keep.tile([PART, HP * 512], U8, name="w4_planes", align_bytes=64)
        h_codes = {}
        h_scales = {}
        for b in range(HP):
            for c in range(2):
                h_codes[b, c] = keep.tile([PART, HALF], U32, name="h_codes%d%d" % (b, c), align_bytes=64)
                h_scales[b, c] = keep.tile([PART, HALF], U8, name="h_scales%d%d" % (b, c), align_bytes=64)
        warm_in = keep.tile([PART, 1], F32, name="warm_in")
        warm_out = keep.tile([PART, 1], F32, name="warm_out")

        banks = {}
        hb_tiles = {}

        def first_product(b, col0, width, passes):
            per_bank = HALF // width
            cols = slice(col0, col0 + width)
            for t in range(4):
                for a in passes:
                    if a == 0 and t % per_bank == 0:
                        banks[b, col0, t // per_bank] = psum.tile([PART, HALF], F32, name="bank", tag="bank")
                    place = (t % per_bank) * width
                    nc.tensor.matmul_mx(
                        out=banks[b, col0, t // per_bank][:, place : place + width],
                        lhsT=w1_codes[b, a][:, t * 128 : (t + 1) * 128].bitcast(FP8X4),
                        lhsT_scale=w1_scales[b, a][:, t * 128 : (t + 1) * 128],
                        rhs=v_codes[a][:, cols].bitcast(FP8X4),
                        rhs_scale=v_scales[4 * a : PART, cols],
                        start=(a == 0),
                        stop=(a == KP - 1),
                    )

        def response_parts(b, col0, width, squares=None):
            per_bank = HALF // width
            rs = work.tile([PART, 4 * width], F32, name="rs", tag="rs")
            u = work.tile([PART, 4 * width], F32, name="u", tag="u")

            def part(n):
                bank = banks[b, col0, n]
                if squares is None:
                    q = work.tile([PART, HALF], F32, name="q", tag="q", bufs=3)[:]
                else:
                    q = squares[:, n * HALF : (n + 1) * HALF]
                nc.scalar.activation(out=q, in_=bank[:], func=ACT.Square)
                nc.scalar.activation(
                    out=rs[:, n * HALF : (n + 1) * HALF], in_=q, func=ACT.Abs_reciprocal_sqrt, bias=1.0, scale=1.0
                )
                for t in range(n * per_bank, (n + 1) * per_bank):
                    place = (t % per_bank) * width
                    nc.vector.scalar_tensor_tensor(
                        out=u[:, t * width : (t + 1) * width],
                        in0=bank[:, place : place + width],
                        scalar=g[:, b, t : t + 1],
                        in1=rs[:, t * width : (t + 1) * width],
                        op0=ALU.mult,
                        op1=ALU.mult,
                    )

            def finish():
                hb = work.tile([PART, 4 * width], BF16, name="hb", tag="hb", align_bytes=64)
                hb_tiles[b, col0] = hb
                nc.vector.tensor_tensor(
                    out=hb[:].rearrange("p (m i t) -> p m t i", i=2, t=4),
                    in0=u[:].rearrange("p (t m i) -> p m t i", t=4, i=2),
                    in1=rs[:].rearrange("p (t m i) -> p m t i", t=4, i=2),
                    op=ALU.mult,
                )

            return part, finish

        def quantise_h(b, col0, width):
            c, lo = divmod(col0, HALF)
            nc.vector.quantize_mx(
                out=h_codes[b, c][:, lo : lo + width].bitcast(FP8X4),
                scales=h_scales[b, c][:, lo : lo + width],
                in_=hb_tiles[b, col0][:],
            )

        def second_product(t, c, b):
            if b == 0:
                banks["e", c, t] = psum.tile([PART, HALF], F32, name="bank", tag="bank")
            col = b * 512 + t * 128
            nc.tensor.matmul_mx(
                out=banks["e", c, t][:],
                lhsT=w4_codes[:, 2 * col : 2 * col + 256].bitcast(FP4X4),
                lhsT_scale=w4_planes[:, col : col + 128],
                rhs=h_codes[b, c][:].bitcast(FP8X4),
                rhs_scale=h_scales[b, c][:],
                start=(b == 0),
                stop=(b == HP - 1),
            )

        with ExitStack() as early_ctx:
            early = early_ctx.enter_context(tc.tile_pool(name="early", bufs=1))
            tab = [early.tile([PART, T], I32, name="tab%d" % a) for a in range(KP)]
            tab_planes = early.tile([PART, T], U8, name="tab_planes")
            w4_raw = early.tile([PART, HP * 1024], U8, name="w4_raw")
            w4_raw_planes = early.tile([PART, HP * 512], U8, name="w4_raw_planes")
            raw = {}
            for b in range(HP):
                for a in range(KP):
                    raw[b, a] = early.tile([PART, 4, 512], F32, name="raw%d%d" % (b, a))
            rounded = {}

            def load_w1(b, a):
                rows = w1[a * 512 : (a + 1) * 512, b * 512 : (b + 1) * 512]
                nc.sync.dma_start(out=raw[b, a][:], in_=rows.rearrange("(p j) r -> p j r", j=4))

            def round_w1(b, a, copy):
                wb = early.tile([PART, 2048], BF16, name="wb", tag="wb", bufs=3, align_bytes=64)
                rounded[b, a] = wb
                copy(
                    out=wb[:].rearrange("p (u e m j) -> p u m j e", u=2, e=2, j=4),
                    in_=raw[b, a][:].rearrange("p j (m u e) -> p u m j e", u=2, e=2),
                )

            def quantise_w1(b, a):
                nc.vector.quantize_mx(
                    out=w1_codes[b, a][:].bitcast(FP8X4), scales=w1_scales[b, a][:], in_=rounded[b, a][:]
                )

            def gather_words(a, lo, hi):
                nc.vector.tensor_copy(
                    out=v_codes[a][:, lo:hi], in_=tab[a][:].bitcast(U32).indirect(idx[:, lo // 16 : hi // 16])
                )

            nc.vector.memset(tab_planes[:].bitcast(I32), 0)
            nc.vector.memset(w4_raw_planes[:].bitcast(I32), 0)
            nc.vector.memset(warm_in[:], 1.0)
            nc.scalar.activation(out=warm_out[:], in_=warm_in[:], func=ACT.Abs_reciprocal_sqrt, bias=1.0, scale=1.0)

            def load_tab(a):
                nc.sync.dma_start(out=tab[a][:], in_=tab_words[a].rearrange("p t i -> p (t i)").bitcast(I32))

            load_w1(0, 0)
            load_w1(0, 1)
            for quad in range(4):
                nc.sync.dma_start(
                    out=tab_planes[32 * quad : 32 * quad + 4 * KP, :].bitcast(I32),
                    in_=tab_scales[:, 4 * quad : 4 * quad + 4, :].bitcast(I32),
                )
            nc.sync.dma_start(idx[:], offs)
            load_w1(0, 2)
            load_tab(0)
            nc.sync.dma_start(
                out=w4_raw[:].bitcast(I32).rearrange("p (b n) -> p b n", b=HP),
                in_=w4_words.bitcast(I32).rearrange("b p n -> p b n"),
            )
            for quad in range(4):
                nc.sync.dma_start(
                    out=w4_raw_planes[32 * quad : 32 * quad + 4, :].bitcast(I32).rearrange("p (b n) -> p b n", b=HP),
                    in_=w4_scales[:, 4 * quad : 4 * quad + 4, :].bitcast(I32).rearrange("b r n -> r b n"),
                )
            load_tab(1)
            load_tab(2)
            nc.sync.dma_start(out=g[:], in_=gain.rearrange("(b p t) -> p b t", b=HP, t=4))
            for a in range(KP):
                load_w1(1, a)
            nc.sync.dma_start(p1[:], pos1)
            nc.sync.dma_start(p2[:], pos2)

            for a in range(KP):
                round_w1(0, a, nc.scalar.copy)
                quantise_w1(0, a)
            nc.vector.tensor_copy(out=v_scales[:], in_=tab_planes[:].indirect(idx[:]))
            for a in range(KP - 1):
                gather_words(a, 0, S)
                first_product(0, 0, HALF, [a])
                first_product(0, HALF, HALF, [a])
            nc.vector.tensor_copy(
                out=w4_codes[:].rearrange("p (b t q e) -> p b t q e", b=HP, t=4, e=2),
                in_=w4_raw[:].rearrange("p (b q t e) -> p b t q e", b=HP, t=4, e=2),
            )
            nc.vector.tensor_copy(
                out=w4_planes[:].rearrange("p (b t q) -> p b t q", b=HP, t=4),
                in_=w4_raw_planes[:].rearrange("p (b q t) -> p b t q", b=HP, t=4),
            )
            gather_words(KP - 1, 0, HALF)
            first_product(0, 0, HALF, [KP - 1])
            gather_words(KP - 1, HALF, S)
            first_product(0, HALF, HALF, [KP - 1])

            part, finish = response_parts(0, 0, HALF)
            for t in range(4):
                part(t)
            round_w1(1, 0, nc.vector.tensor_copy)
            round_w1(1, 1, nc.scalar.copy)
            finish()
            quantise_w1(1, 0)
            round_w1(1, 2, nc.scalar.copy)
            quantise_h(0, 0, HALF)
            quantise_w1(1, 1)
            part, finish = response_parts(0, HALF, HALF)
            part(0)
            quantise_w1(1, 2)
            for t in range(1, 4):
                part(t)
            finish()

        late = ctx.enter_context(tc.tile_pool(name="late", bufs=1))
        base_rows = base.rearrange("(p t) m -> p t m", t=4)
        out_rows = out_0.rearrange("(p t) m -> p t m", t=4)
        base_tiles = []
        for m0, width in PAIR_CHUNKS:
            tile = late.tile([PART, 4, width], F32, name="base%d" % m0)
            nc.sync.dma_start(out=tile[:], in_=base_rows[:, :, m0 : m0 + width])
            base_tiles.append(tile)

        first_product(1, 0, HALF, range(KP))
        part, finish = response_parts(1, 0, HALF)
        part(0)
        quantise_h(0, HALF, HALF)
        for t in range(1, 4):
            part(t)
        finish()
        first_product(1, HALF, 256, range(KP))
        first_product(1, HALF + 256, 256, range(KP))
        part, finish = response_parts(1, HALF, 256)
        part(0)
        quantise_h(1, 0, HALF)
        for t in range(4):
            for b in range(HP):
                second_product(t, 0, b)
        part(1)
        finish()
        q_last = tail.tile([PART, 4 * S], F32, name="q_last", offset=0)
        part, finish = response_parts(1, HALF + 256, 256, q_last)
        part(0)
        quantise_h(1, HALF, 256)
        part(1)
        finish()
        for t in range(4):
            second_product(t, 1, 0)
        quantise_h(1, HALF + 256, 256)
        g2 = []
        for t in range(4):
            g2.append(tail.tile([PART, S], F32, name="g2_%d" % t, offset=t * S * 4))
            nc.scalar.activation(out=g2[t][:, 0:HALF], in_=banks["e", 0, t][:], func=ACT.Silu)
        for t in range(4):
            second_product(t, 1, 1)
            nc.scalar.activation(out=g2[t][:, HALF:S], in_=banks["e", 1, t][:], func=ACT.Silu)

        y_codes = late.tile([PART, P], U32, name="y_codes", align_bytes=64)
        y_scales = late.tile([PART, P], U8, name="y_scales", align_bytes=64)
        words_out = out_1[0].rearrange("p m t -> p (m t)").bitcast(I32)
        pending = []
        for chunk, (m0, width) in enumerate(PAIR_CHUNKS):
            left = late.tile([PART, 4, width], F32, name="left%d" % m0)
            right = late.tile([PART, 4, width], F32, name="right%d" % m0)
            y = late.tile([PART, 4, width], F32, name="y%d" % m0)
            yb = late.tile([PART, 4 * width], BF16, name="yb%d" % m0, align_bytes=64)
            cols = slice(m0 // 16, (m0 + width) // 16)
            for t in range(4):
                given = base_tiles[chunk][:, t, :]
                nc.vector.tensor_tensor(out=left[:, t, :], in0=g2[t][:].indirect(p1[:, cols]), in1=given, op=ALU.subtract)
                nc.vector.tensor_tensor(out=right[:, t, :], in0=g2[t][:].indirect(p2[:, cols]), in1=given, op=ALU.subtract)
            for step in pending:
                step()
            nc.vector.tensor_tensor(out=y[:], in0=left[:], in1=right[:], op=ALU.min)
            nc.sync.dma_start(out=out_rows[:, :, m0 : m0 + width], in_=y[:])
            copy = nc.vector.tensor_copy if chunk == len(PAIR_CHUNKS) - 1 else nc.scalar.copy
            copy(
                out=yb[:].rearrange("p (m i t) -> p m t i", i=2, t=4),
                in_=y[:].rearrange("p t (m i) -> p m t i", i=2),
            )

            def planes(m0=m0, width=width, yb=yb):
                done = 0
                for piece in (256, 128):
                    if done + piece <= width:
                        lo = m0 + done
                        nc.vector.quantize_mx(
                            out=y_codes[:, lo : lo + piece].bitcast(FP8X4),
                            scales=y_scales[:, lo : lo + piece],
                            in_=yb[:, 4 * done : 4 * (done + piece)],
                        )
                        done = done + piece
                nc.sync.dma_start(out=words_out[:, m0 : m0 + width], in_=y_codes[:, m0 : m0 + width].bitcast(I32))

            pending = [planes]
        for step in pending:
            step()
        for quad in range(4):
            queue = nc.sync if quad < 2 else nc.scalar
            queue.dma_start(
                out=out_2[0][4 * quad : 4 * quad + 4, :].bitcast(I32),
                in_=y_scales[32 * quad : 32 * quad + 4, :].bitcast(I32),
            )
